import numpy as np, ml_dtypes
CORES = [7,15,23,39,47,63,71,79,87,95,119,127]
N = 12
DEG, TK, TIMES = 3, 256, 2
MASK = [[0,6,10],[1,4,9],[2,6,8],[1,3,6],[3,4,7],[1,3,5],[5,6,10],[3,5,7],[2,8,9],[6,9,10],[4,5,10],[3,5,11]]
def setup_inputs(rng):
    return {"x": rng.standard_normal((N, 128, TK), dtype=np.float32).astype(ml_dtypes.bfloat16), "w": (rng.standard_normal((N, 128, DEG * 128), dtype=np.float32) / np.float32(np.sqrt(128 * DEG / 2))).astype(ml_dtypes.bfloat16)}
def setup_inputs_big(rng):
    d = setup_inputs(rng)
    for k in ("x",): d[k] = (d[k].astype(np.float32) * 1048576.0).astype(d[k].dtype)
    return d
def setup_inputs_small(rng):
    d = setup_inputs(rng)
    for k in ("x",): d[k] = (d[k].astype(np.float32) * (1 / 1048576.0)).astype(d[k].dtype)
    return d
def setup_inputs_apart(rng):
    d = setup_inputs(rng)
    f = (10.0 ** rng.permutation(np.linspace(-1.5, 1.5, N))).astype(np.float32).reshape(N, 1, 1)
    for k in ("x",): d[k] = (d[k].astype(np.float32) * f).astype(d[k].dtype)
    return d
def reference(x, w):
    X, W = x.astype(np.float64), w.astype(np.float64)
    h = list(X)
    for _ in range(TIMES):
        h = [np.maximum(sum(W[r][:, 128 * i:128 * i + 128].T @ h[j] for i, j in enumerate(MASK[r])), 0.0) for r in range(N)]
    return {"y": np.stack(h).astype(ml_dtypes.bfloat16)}

from concourse.bass import DstId, RemoteDMATransfer
from concourse.mybir import AluOpType

N, DEG, TK, P, TIMES = 12, 3, 256, 128, 2

SCRATCH = {
    "wsb": ("sbuf", [P, DEG * P], "bfloat16"),
    "zero": ("sbuf", [P, TK], "float32"),
    "own0": ("sbuf", [P, TK], "bfloat16"),
    "own1": ("sbuf", [P, TK], "bfloat16"),
    "own2": ("sbuf", [P, TK], "bfloat16"),
    "ps0": ("psum", [P, 512], "float32"),
    "ps1": ("psum", [P, 512], "float32"),
}
for _t in range(TIMES):
    for _i in range(DEG):
        SCRATCH["in%d_%d" % (_t, _i)] = ("sbuf", [P, TK], "bfloat16")

SEMAPHORES = ["xl", "wl", "zf", "mm0", "mm1", "mx0", "mx1", "st", "left"] + [
    "got%d_%d" % (_t, _j) for _t in range(TIMES) for _j in range(N)]

_CACHE = {}


def _ports(topo, src, dst):
    a, b, d = topo.chip(src), topo.chip(dst), topo.die(src)
    if a == b:
        return []
    if topo.mates(a, b):
        return [("mate", a, d)]
    if topo.same_plane(a, b):
        return [("out", a, d), ("in", b, d)]
    m = [c for c in range(topo.CHIPS) if topo.mates(a, c)][0]
    return [("mate", a, d), ("out", m, d), ("in", b, d)]


def _slots(edges, first, count, ports):
    used, out = set(), {}

    def rec(k):
        if k == len(edges):
            return True
        j, r = edges[k]
        for s in range(first[j], first[j] + count[j]):
            keys = [("snd", j, s), ("rcv", r, s)] + [(p, s) for p in ports[(j, r)]]
            if any(q in used for q in keys):
                continue
            used.update(keys)
            out[(j, r)] = s
            if rec(k + 1):
                return True
            used.difference_update(keys)
            del out[(j, r)]
        return False

    return out if rec(0) else None


def _plan(mask, cores, topo):
    n = len(mask)
    outs = [[r for r in range(n) if r != j and j in mask[r]] for j in range(n)]
    deg = [len(o) for o in outs]
    edges = [(j, r) for j in range(n) for r in outs[j]]
    ports = {(j, r): _ports(topo, cores[j], cores[r]) for j, r in edges}
    free = {e: [] for e in edges}
    e0 = sorted(edges, key=lambda e: (-deg[e[1]], e[0]))
    s0 = _slots(e0, [0] * n, deg, ports) or _slots(e0, [0] * n, deg, free)
    have = [1 + max([s0[(j, r)] for j in mask[r] if j != r] + [-1]) for r in range(n)]
    e1 = sorted(edges, key=lambda e: (-(have[e[0]] + deg[e[0]]), e[0], e[1]))
    s1 = _slots(e1, have, deg, ports) or _slots(e1, have, deg, free)
    return {"outs": outs, "slot": [s0, s1]}


def _count(m):
    return sum((m >> b) & 1 for b in range(16))


def rank_program(g, core, T, topo):
    rank = T.rank_of(core)
    if rank is None:
        return
    mask, cores, sem = T.tables["MASK"], list(T.cores), T.sem
    if "plan" not in _CACHE:
        _CACHE["plan"] = _plan(mask, cores, topo)
    plan = _CACHE["plan"]
    row = mask[rank]

    g.sync.dma_start(T.own0[:], T.x[:]).then_inc(sem.xl, 16)
    g.sync.dma_start(T.wsb[:], T.w[:]).then_inc(sem.wl, 16)
    g.vector.memset(T.zero[:], 0.0).then_inc(sem.zf, 1)

    left = 0
    for t in range(TIMES):
        slot = plan["slot"][t]
        dests = sorted(plan["outs"][rank], key=lambda r: slot[(rank, r)])
        if not dests:
            continue
        if t == 0:
            g.wait_ge(sem.xl, 16)
        else:
            g.wait_ge(sem["mx%d" % (t - 1)], 1)
        src, got = T["own%d" % t], sem["got%d_%d" % (t, rank)]
        for r in dests:
            assert topo.may_write(core, cores[r])
        lands = [T["in%d_%d" % (t, mask[r].index(rank))] for r in dests]
        if t < TIMES - 1 or len(dests) == 1:
            for r, land in zip(dests, lands):
                rid, pid, _ = topo.addr(cores[r])
                m = topo.mask(core, cores[r])
                g.remote_dma(out_ap=land[:], in_ap=src[:], remote_sem=got, local_sem=sem.left,
                             pid=pid, routing_id=rid, dma_engine_mask=m)
                left += _count(m)
        else:
            m = topo.mask(core, cores[dests[0]])
            for r in dests:
                m &= topo.mask(core, cores[r])
            ids = [DstId(rid=topo.addr(cores[r])[0], pnc=topo.addr(cores[r])[1]) for r in dests]
            g.remote_dma_fused([RemoteDMATransfer(dst_ids=ids, dma_engine_mask=m, remote_sem=got, srcs=[src[:]],
                                                  dsts=[land[:] for land in lands], alu_op=0)], local_sem=sem.left)
            left += _count(m)
    if left:
        g.wait_ge(sem.left, left)

    g.vector.wait_ge(sem.zf, 1)
    for t in range(TIMES):
        slot = plan["slot"][t]
        ps = T["ps%d" % t][:, 0:TK]
        order = sorted(range(DEG), key=lambda i: -1 if row[i] == rank else slot[(row[i], rank)])
        for k, i in enumerate(order):
            j = row[i]
            if k == 0 and t == 0:
                g.tensor.wait_ge(sem.wl, 16)
            if j == rank:
                if t == 0:
                    g.tensor.wait_ge(sem.xl, 16)
                else:
                    g.tensor.wait_ge(sem["mx%d" % (t - 1)], 1)
                rhs = T["own%d" % t]
            else:
                m = topo.mask(cores[j], core)
                if t == TIMES - 1:
                    for r in plan["outs"][j]:
                        m &= topo.mask(cores[j], cores[r])
                g.tensor.wait_ge(sem["got%d_%d" % (t, j)], _count(m))
                rhs = T["in%d_%d" % (t, i)]
            g.tensor.matmul(ps, T.wsb[:, P * i:P * (i + 1)], rhs[:], start=(k == 0),
                            stop=(k == DEG - 1)).then_inc(sem["mm%d" % t], 1)
        g.vector.wait_ge(sem["mm%d" % t], DEG)
        g.vector.tensor_tensor(T["own%d" % (t + 1)][:], ps, T.zero[:], AluOpType.max).then_inc(sem["mx%d" % t], 1)

    g.sync.wait_ge(sem["mx%d" % (TIMES - 1)], 1)
    g.sync.dma_start(T.y[:], T["own%d" % TIMES][:]).then_inc(sem.st, 16)
    g.sync.wait_ge(sem.st, 16)
